import numpy as np, ml_dtypes
CORES = [40,64,80,88,96,104,120,144]
N = 8
T, W, CAP = 4096, 256, 128
def entries(a): return a.T.reshape(-1)
def pack(v, P): return np.ascontiguousarray(np.asarray(v, np.int32).reshape(-1, P).T)
def lists(rng, how):
    L = rng.integers(0, T, (N, N, CAP))
    if how == "alike": L[:] = rng.integers(0, T, (N, N, 1))
    if how == "distinct": L = np.stack([np.stack([rng.permutation(T)[:CAP] for d in range(N)]) for r in range(N)])
    if how == "sorted": L = np.sort(L, axis=2)
    if how == "edge": L = np.where(rng.random((N, N, CAP)) < 0.5, 0, T - 1)
    return {"l": np.stack([pack(L[r].reshape(-1), 128) for r in range(N)])}
def setup_inputs(rng):
    return dict({"x": rng.standard_normal((N, T, W), dtype=np.float32).astype(ml_dtypes.bfloat16)}, **lists(rng, "uniform"))
def setup_inputs_alike(rng):
    d = setup_inputs(rng); d.update(lists(rng, "alike"))
    for k in ("x",): d[k] = (d[k].astype(np.float32) * 1048576.0).astype(d[k].dtype)
    return d
def setup_inputs_distinct(rng):
    d = setup_inputs(rng); d.update(lists(rng, "distinct"))
    for k in ("x",): d[k] = (d[k].astype(np.float32) * (1 / 1024.0)).astype(d[k].dtype)
    return d
def setup_inputs_edge(rng):
    d = setup_inputs(rng); d.update(lists(rng, "edge"))
    return d
def setup_inputs_sorted(rng):
    d = setup_inputs(rng); d.update(lists(rng, "sorted"))
    return d
def check_inputs(x):
    bad = []
    if x["l"].min() < 0 or x["l"].max() >= T: bad.append("l out of range")
    return bad
def reference(x, l):
    y = np.zeros((N, N * CAP, W), x.dtype)
    for r in range(N):
        L = entries(l[r])
        for d in range(N): y[d][CAP * r:CAP * r + CAP] = x[r][L[CAP * d:CAP * d + CAP]]
    return {"y": y}

@@ -1,0 +1,163 @@
+from concourse.bass import DstId, RemoteDMATransfer, IndirectOffsetOnAxis
+
+N, ROWS, W, CAP = 8, 4096, 256, 128
+WORLD = 256
+
+PLAN = [("g", "x0"), ("g", "x1"), ("g", "x2"), ("s", ["x0", "x1"]),
+        ("g", "x3"), ("g", "s1"), ("s", ["x2", "x3"]),
+        ("g", "s2"), ("s", ["s1"]),
+        ("g", "s3"), ("s", ["s2"]), ("s", ["s3"]),
+        ("g", "own")]
+BLOCKS = [b for op, b in PLAN if op == "g"]
+NHELP = 2
+STORES = {"sync": ["x0", "s1", "x2", "s3"], "scalar": ["x1", "x3", "s2", "own"]}
+
+SCRATCH = {
+    "lsb": ("sbuf", [128, N], "int32"),
+    "gat": ("sbuf", [128, N * W], "bfloat16"),
+    "land": ("dram", [N, 128, W], "bfloat16"),
+}
+SEMAPHORES = (["lld", "sent", "sts", "sta"] + ["g%d" % k for k in range(N)] + ["arr%d" % k for k in range(N)]
+              + ["hin%d" % k for k in range(4 // NHELP)])
+
+
+def bits(mask):
+    return [1 << b for b in range(16) if (mask >> b) & 1]
+
+
+def join(bs):
+    m = 0
+    for b in bs:
+        m |= b
+    return m
+
+
+def classes(cores, topo):
+    cls = []
+    for r, c in enumerate(cores):
+        for k in cls:
+            if topo.may_write(cores[k[0]], c) and topo.may_write(c, cores[k[0]]):
+                k.append(r)
+                break
+        else:
+            cls.append([r])
+    return cls
+
+
+def dest(r, block, cls):
+    mine = [k for k in cls if r in k][0]
+    other = [k for k in cls if r not in k][0]
+    if block == "own":
+        return r
+    k = int(block[1:])
+    to = mine if block[0] == "s" else other
+    return to[(mine.index(r) + k) % len(to)]
+
+
+def helpers(r, cores, cls, topo):
+    c = cores[r]
+    far = [cores[dest(r, b, cls)] for b in BLOCKS if b[0] == "x"]
+    hs = [h for h in range(WORLD) if h != c and topo.host(h) == topo.host(c) and topo.chip(h) == topo.chip(c)
+          and all(topo.may_write(h, f) for f in far)]
+    hs = [h for h in hs if topo.die(h) != topo.die(c)] + [h for h in hs if topo.die(h) == topo.die(c)]
+    return hs[:NHELP]
+
+
+def first_hops(r, cores, cls, topo):
+    c = cores[r]
+    hs = helpers(r, cores, cls, topo)
+    tgt = {}
+    for b in BLOCKS:
+        if b[0] == "x":
+            tgt[b] = hs[int(b[1:]) % NHELP]
+        elif b[0] == "s":
+            tgt[b] = cores[dest(r, b, cls)]
+    pool = None
+    for t in tgt.values():
+        pool = topo.mask(c, t) if pool is None else pool & topo.mask(c, t)
+    pool = bits(pool)
+    out = {}
+    for op, bs in PLAN:
+        if op != "s":
+            continue
+        per = 1
+        while per * 2 * len(bs) <= len(pool):
+            per *= 2
+        for j, b in enumerate(bs):
+            out[b] = (tgt[b], join(pool[j * per:(j + 1) * per]))
+    return out
+
+
+def rank_program(g, core, T, topo):
+    cores = list(T.cores)
+    cls = classes(cores, topo)
+    rank = T.rank_of(core)
+
+    if rank is None:
+        own = [r for r in range(N) if topo.host(cores[r]) == topo.host(core) and topo.chip(cores[r]) == topo.chip(core)]
+        if not own or core not in helpers(own[0], cores, cls, topo):
+            return
+        r = own[0]
+        hops = first_hops(r, cores, cls, topo)
+        sent = 0
+        for b in BLOCKS:
+            if b[0] != "x" or hops[b][0] != core:
+                continue
+            d = dest(r, b, cls)
+            rid, pid = topo.addr(cores[d], core)
+            m = topo.mask(core, cores[d])
+            g.wait_ge(T.sem["hin%d" % (int(b[1:]) // NHELP)], len(bits(hops[b][1])))
+            g.remote_dma(out_ap=T.land[r], in_ap=T.land[d], remote_sem=T.sem["arr%d" % r], local_sem=T.sem.sent,
+                         pid=pid, routing_id=rid, dma_engine_mask=m)
+            sent += len(bits(m))
+        g.wait_ge(T.sem.sent, sent)
+        return
+
+    g.sync.dma_start(T.lsb[:], T.l[:]).then_inc(T.sem.lld, 16)
+    g.wait_ge(T.sem.lld, 16)
+    hops = first_hops(rank, cores, cls, topo)
+    sent = 0
+    for op, what in PLAN:
+        if op == "g":
+            k, d = BLOCKS.index(what), dest(rank, what, cls)
+            g.indirect_dma_start(T.gat[:, k * W:(k + 1) * W], None, T.x[:],
+                                 IndirectOffsetOnAxis(ap=T.lsb[:, d:d + 1], axis=0),
+                                 bounds_check=ROWS - 1).then_inc(T.sem["g%d" % k], 16)
+            continue
+        trs = []
+        for b in what:
+            k, d = BLOCKS.index(b), dest(rank, b, cls)
+            g.wait_ge(T.sem["g%d" % k], 16)
+            to, m = hops[b]
+            rid, pid = topo.addr(to, core)
+            if b[0] == "x":
+                dst, sem = T.land[d], T.sem["hin%d" % (int(b[1:]) // NHELP)]
+            else:
+                dst, sem = T.land[rank], T.sem["arr%d" % rank]
+            trs.append((rid, pid, m, sem, T.gat[:, k * W:(k + 1) * W], dst))
+            sent += len(bits(m))
+        if len(trs) == 1:
+            rid, pid, m, sem, src, dst = trs[0]
+            g.remote_dma(out_ap=dst, in_ap=src, remote_sem=sem, local_sem=T.sem.sent, pid=pid, routing_id=rid,
+                         dma_engine_mask=m)
+        else:
+            g.remote_dma_fused([RemoteDMATransfer(dst_ids=[DstId(rid=rid, pnc=pid)], dma_engine_mask=m, remote_sem=sem,
+                                                  src=src, dst=dst) for rid, pid, m, sem, src, dst in trs],
+                               local_sem=T.sem.sent)
+
+    for q, sem, order in ((g.sync, T.sem.sts, STORES["sync"]), (g.scalar, T.sem.sta, STORES["scalar"])):
+        for b in order:
+            if b == "own":
+                k = BLOCKS.index(b)
+                q.wait_ge(T.sem["g%d" % k], 16)
+                q.dma_start(T.y[rank * CAP:(rank + 1) * CAP, :], T.gat[:, k * W:(k + 1) * W]).then_inc(sem, 16)
+                continue
+            r = [s for s in range(N) if s != rank and dest(s, b, cls) == rank][0]
+            to, m = first_hops(r, cores, cls, topo)[b]
+            if b[0] == "x":
+                m = topo.mask(to, core)
+            q.wait_ge(T.sem["arr%d" % r], len(bits(m)))
+            q.dma_start(T.y[r * CAP:(r + 1) * CAP, :], T.land[r]).then_inc(sem, 16)
+    g.wait_ge(T.sem.sent, sent)
+    g.wait_ge(T.sem.sts, 16 * len(STORES["sync"]))
+    g.wait_ge(T.sem.sta, 16 * len(STORES["scalar"]))

@@ -6,8 +6,8 @@ WORLD = 256
 PLAN = [("g", "x0"), ("g", "x1"), ("g", "x2"), ("s", ["x0", "x1"]),
         ("g", "x3"), ("g", "s1"), ("s", ["x2", "x3"]),
         ("g", "s2"), ("s", ["s1"]),
-        ("g", "s3"), ("s", ["s2"]), ("s", ["s3"]),
-        ("g", "own")]
+        ("g", "s3"), ("s", ["s2"]),
+        ("g", "own"), ("s", ["s3"])]
 BLOCKS = [b for op, b in PLAN if op == "g"]
 NHELP = 2
 STORES = {"sync": ["x0", "s1", "x2", "s3"], "scalar": ["x1", "x3", "s2", "own"]}
@@ -17,7 +17,7 @@ SCRATCH = {
     "gat": ("sbuf", [128, N * W], "bfloat16"),
     "land": ("dram", [N, 128, W], "bfloat16"),
 }
-SEMAPHORES = (["lld", "sent", "sts", "sta"] + ["g%d" % k for k in range(N)] + ["arr%d" % k for k in range(N)]
+SEMAPHORES = (["lld", "lg", "sent", "sts", "sta"] + ["g%d" % k for k in range(N)] + ["arr%d" % k for k in range(N)]
               + ["hin%d" % k for k in range(4 // NHELP)])
 
 
@@ -51,7 +51,7 @@ def dest(r, block, cls):
         return r
     k = int(block[1:])
     to = mine if block[0] == "s" else other
-    return to[(mine.index(r) + k) % len(to)]
+    return to[mine.index(r) ^ k]
 
 
 def helpers(r, cores, cls, topo):
@@ -113,25 +113,34 @@ def rank_program(g, core, T, topo):
         g.wait_ge(T.sem.sent, sent)
         return
 
-    g.sync.dma_start(T.lsb[:], T.l[:]).then_inc(T.sem.lld, 16)
+    half = N // 2
+    a = dest(rank, BLOCKS[0], cls) // half * half
+    assert dest(rank, BLOCKS[1], cls) // half * half == a
+    b = half - a
+    g.sync.dma_start(T.lsb[:, a:a + half], T.l[:, a:a + half]).then_inc(T.sem.lld, 16)
+    g.dma_start(T.lsb[:, b:b + half], T.l[:, b:b + half]).then_inc(T.sem.lg, 16)
     g.wait_ge(T.sem.lld, 16)
+    late = True
     hops = first_hops(rank, cores, cls, topo)
     sent = 0
     for op, what in PLAN:
         if op == "g":
             k, d = BLOCKS.index(what), dest(rank, what, cls)
+            if late and b <= d < b + half:
+                g.wait_ge(T.sem.lg, 16)
+                late = False
             g.indirect_dma_start(T.gat[:, k * W:(k + 1) * W], None, T.x[:],
                                  IndirectOffsetOnAxis(ap=T.lsb[:, d:d + 1], axis=0),
                                  bounds_check=ROWS - 1).then_inc(T.sem["g%d" % k], 16)
             continue
         trs = []
-        for b in what:
-            k, d = BLOCKS.index(b), dest(rank, b, cls)
+        for blk in what:
+            k, d = BLOCKS.index(blk), dest(rank, blk, cls)
             g.wait_ge(T.sem["g%d" % k], 16)
-            to, m = hops[b]
+            to, m = hops[blk]
             rid, pid = topo.addr(to, core)
-            if b[0] == "x":
-                dst, sem = T.land[d], T.sem["hin%d" % (int(b[1:]) // NHELP)]
+            if blk[0] == "x":
+                dst, sem = T.land[d], T.sem["hin%d" % (int(blk[1:]) // NHELP)]
             else:
                 dst, sem = T.land[rank], T.sem["arr%d" % rank]
             trs.append((rid, pid, m, sem, T.gat[:, k * W:(k + 1) * W], dst))
@@ -146,15 +155,15 @@ def rank_program(g, core, T, topo):
                                local_sem=T.sem.sent)
 
     for q, sem, order in ((g.sync, T.sem.sts, STORES["sync"]), (g.scalar, T.sem.sta, STORES["scalar"])):
-        for b in order:
-            if b == "own":
-                k = BLOCKS.index(b)
+        for blk in order:
+            if blk == "own":
+                k = BLOCKS.index(blk)
                 q.wait_ge(T.sem["g%d" % k], 16)
                 q.dma_start(T.y[rank * CAP:(rank + 1) * CAP, :], T.gat[:, k * W:(k + 1) * W]).then_inc(sem, 16)
                 continue
-            r = [s for s in range(N) if s != rank and dest(s, b, cls) == rank][0]
-            to, m = first_hops(r, cores, cls, topo)[b]
-            if b[0] == "x":
+            r = [s for s in range(N) if s != rank and dest(s, blk, cls) == rank][0]
+            to, m = first_hops(r, cores, cls, topo)[blk]
+            if blk[0] == "x":
                 m = topo.mask(to, core)
             q.wait_ge(T.sem["arr%d" % r], len(bits(m)))
             q.dma_start(T.y[r * CAP:(r + 1) * CAP, :], T.land[r]).then_inc(sem, 16)

@@ -1,24 +1,49 @@
 from concourse.bass import DstId, RemoteDMATransfer, IndirectOffsetOnAxis
+from concourse.mybir import AluOpType
 
 N, ROWS, W, CAP = 8, 4096, 256, 128
 WORLD = 256
 
 PLAN = [("g", "x0"), ("g", "x1"), ("g", "x2"), ("s", ["x0", "x1"]),
         ("g", "x3"), ("g", "s1"), ("s", ["x2", "x3"]),
-        ("g", "s2"), ("s", ["s1"]),
-        ("g", "s3"), ("s", ["s2"]),
-        ("g", "own"), ("s", ["s3"])]
-BLOCKS = [b for op, b in PLAN if op == "g"]
+        ("g", "s2"), ("s", ["s1"]), ("s", ["s2"]), ("s", ["s3"])]
+GATH = [b for op, b in PLAN if op == "g"]
+COMP = ["s3", "own"]
+BLOCKS = GATH + COMP
 NHELP = 2
 STORES = {"sync": ["x0", "s1", "x2", "s3"], "scalar": ["x1", "x3", "s2", "own"]}
 
+NCH = 8
+CR = ROWS // NCH
+SL = CR // 128
+CW = SL * W
+NB = 4
+H = W // 128
+OC = CAP // 16
+
 SCRATCH = {
     "lsb": ("sbuf", [128, N], "int32"),
-    "gat": ("sbuf", [128, N * W], "bfloat16"),
+    "gat": ("sbuf", [128, len(GATH) * W], "bfloat16"),
+    "xs": ("sbuf", [128, NCH * CW], "bfloat16"),
+    "xt": ("sbuf", [128, H * ROWS], "bfloat16"),
+    "gt": ("sbuf", [128, len(COMP) * W], "bfloat16"),
+    "cb": ("sbuf", [128, len(COMP) * W], "bfloat16"),
+    "iot": ("sbuf", [128, 128], "int32"), "iob": ("sbuf", [128, OC], "int32"),
+    "t15": ("sbuf", [128, 128], "int32"), "m4": ("sbuf", [128, OC], "int32"),
+    "ident": ("sbuf", [128, 128], "bfloat16"), "sel": ("sbuf", [128, 128], "float32"), "mhi": ("sbuf", [128, OC], "float32"),
+    "t1": ("sbuf", [128, N], "int32"), "t2": ("sbuf", [128, N], "int32"), "t3": ("sbuf", [128, N], "int32"),
+    "f2": ("sbuf", [128, N], "float32"), "f13": ("sbuf", [128, N], "float32"), "off": ("sbuf", [128, N], "float32"),
+    "lmat": ("sbuf", [128, len(COMP) * OC], "float32"), "offs": ("sbuf", [128, len(COMP) * OC], "uint16"),
+    "pt": ("psum", [128, NB * CW], "bfloat16"),
+    "po": ("psum", [128, 512], "float32"),
+    "pb": ("psum", [128, len(COMP) * CW], "bfloat16"),
     "land": ("dram", [N, 128, W], "bfloat16"),
 }
-SEMAPHORES = (["lld", "lg", "sent", "sts", "sta"] + ["g%d" % k for k in range(N)] + ["arr%d" % k for k in range(N)]
-              + ["hin%d" % k for k in range(4 // NHELP)])
+SEMAPHORES = (["lld", "lg", "sent", "sts", "sta", "cio", "cid", "va", "lm", "mo", "of"]
+              + ["g%d" % k for k in range(len(GATH))] + ["arr%d" % k for k in range(N)]
+              + ["hin%d" % k for k in range(4 // NHELP)]
+              + ["%s%d" % (n, k) for n in ("xl", "tp", "ev") for k in range(NCH)]
+              + ["%s%d" % (n, k) for n in ("gq", "bt", "cb") for k in range(len(COMP))])
 
 
 def bits(mask):
@@ -88,6 +113,70 @@ def first_hops(r, cores, cls, topo):
     return out
 
 
+def compute_way(g, T, lists):
+    V, P, A, S = g.vector, g.tensor, AluOpType, T.sem
+    nq = len(lists)
+    V.wait_ge(S["cio"], 2)
+    V.tensor_scalar(T.ident[:], T.iot[:], 128, None, A.is_equal).then_inc(S["cid"], 1)
+    V.tensor_scalar(T.t15[:], T.iot[:], 15, None, A.bitwise_and).then_inc(S["va"], 1)
+    V.tensor_scalar(T.m4[:], T.iob[:], 4, None, A.logical_shift_right).then_inc(S["va"], 1)
+    V.wait_ge(S["va"], 2)
+    V.tensor_scalar(T.sel[:], T.t15[:], 0, None, A.is_equal).then_inc(S["lm"], 1)
+    V.tensor_scalar(T.mhi[:], T.m4[:], 8, None, A.is_equal).then_inc(S["va"], 1)
+    V.wait_ge(S["lld"], 16)
+    V.wait_ge(S["lg"], 16)
+    V.tensor_scalar(T.t1[:], T.lsb[:], ROWS - CR, None, A.bitwise_and).then_inc(S["va"], 1)
+    V.tensor_scalar(T.t2[:], T.lsb[:], SL - 1, None, A.bitwise_and).then_inc(S["va"], 1)
+    V.tensor_scalar(T.t3[:], T.lsb[:], SL.bit_length() - 1, 127, A.logical_shift_right, A.bitwise_and).then_inc(S["va"], 1)
+    V.wait_ge(S["va"], 6)
+    V.tensor_scalar(T.f2[:], T.t2[:], 128, None, A.mult).then_inc(S["va"], 1)
+    V.tensor_tensor(T.f13[:], T.t1[:], T.t3[:], A.add).then_inc(S["va"], 1)
+    V.wait_ge(S["va"], 8)
+    V.tensor_tensor(T.off[:], T.f13[:], T.f2[:], A.add).then_inc(S["va"], 1)
+    V.wait_ge(S["va"], 9)
+    for q, d in enumerate(lists):
+        V.tensor_scalar(T.lmat[:, q * OC:(q + 1) * OC], T.mhi[:], T.off[:, d:d + 1], None, A.mult).then_inc(S["lm"], 1)
+
+    P.wait_ge(S["cid"], 1)
+    for k in range(NCH):
+        P.wait_ge(S["xl%d" % k], 16)
+        if k >= NB:
+            P.wait_ge(S["ev%d" % (k - NB)], H)
+        for h in range(H):
+            for s in range(SL):
+                o = (k % NB) * CW + (h * SL + s) * 128
+                i = k * CW + s * W + h * 128
+                P.transpose(T.pt[:, o:o + 128], T.xs[:, i:i + 128], T.ident[:]).then_inc(S["tp%d" % k], 1)
+        if k == 1:
+            P.wait_ge(S["lm"], 1 + nq)
+            P.matmul(T.po[:, 0:nq * OC], T.sel[:], T.lmat[:], True, True).then_inc(S["mo"], 1)
+    for q in range(nq):
+        P.wait_ge(S["gq%d" % q], H)
+        for h in range(H):
+            P.transpose(T.pb[:, q * CW + h * 128:q * CW + (h + 1) * 128], T.gt[:, (q * H + h) * 128:(q * H + h + 1) * 128],
+                        T.ident[:]).then_inc(S["bt%d" % q], 1)
+
+    for k in range(NCH):
+        V.wait_ge(S["tp%d" % k], H * SL)
+        for h in range(H):
+            V.tensor_copy(T.xt[:, h * ROWS + k * CR:h * ROWS + (k + 1) * CR],
+                          T.pt[:, (k % NB) * CW + h * CR:(k % NB) * CW + (h + 1) * CR]).then_inc(S["ev%d" % k], 1)
+        if k == 1:
+            V.wait_ge(S["mo"], 1)
+            V.tensor_copy(T.offs[:], T.po[:, 0:nq * OC]).then_inc(S["of"], 1)
+    for k in range(NCH):
+        V.wait_ge(S["ev%d" % k], H)
+    V.wait_ge(S["of"], 1)
+    for q in range(nq):
+        for h in range(H):
+            V.tensor_copy(T.gt[:, (q * H + h) * 128:(q * H + h + 1) * 128],
+                          T.xt[:, h * ROWS:(h + 1) * ROWS].indirect(T.offs[:, q * OC:(q + 1) * OC])
+                          ).then_inc(S["gq%d" % q], 1)
+    for q in range(nq):
+        V.wait_ge(S["bt%d" % q], H)
+        V.tensor_copy(T.cb[:, q * W:(q + 1) * W], T.pb[:, q * CW:q * CW + W]).then_inc(S["cb%d" % q], 1)
+
+
 def rank_program(g, core, T, topo):
     cores = list(T.cores)
     cls = classes(cores, topo)
@@ -114,18 +203,25 @@ def rank_program(g, core, T, topo):
         return
 
     half = N // 2
-    a = dest(rank, BLOCKS[0], cls) // half * half
-    assert dest(rank, BLOCKS[1], cls) // half * half == a
+    a = dest(rank, GATH[0], cls) // half * half
+    assert dest(rank, GATH[1], cls) // half * half == a
     b = half - a
     g.sync.dma_start(T.lsb[:, a:a + half], T.l[:, a:a + half]).then_inc(T.sem.lld, 16)
     g.dma_start(T.lsb[:, b:b + half], T.l[:, b:b + half]).then_inc(T.sem.lg, 16)
+    for k in range(NCH):
+        q = g.scalar if k % 2 == 0 else g.sync
+        q.dma_start(T.xs[:, k * CW:(k + 1) * CW], T.x[CR * k:CR * (k + 1), :]).then_inc(T.sem["xl%d" % k], 16)
+    g.iota(T.iot[:], [[-1, 128]], 128, 1).then_inc(T.sem["cio"], 1)
+    g.iota(T.iob[:], [[-16, OC]], 128, 1).then_inc(T.sem["cio"], 1)
+    compute_way(g, T, [dest(rank, blk, cls) for blk in COMP])
+
     g.wait_ge(T.sem.lld, 16)
     late = True
     hops = first_hops(rank, cores, cls, topo)
     sent = 0
     for op, what in PLAN:
         if op == "g":
-            k, d = BLOCKS.index(what), dest(rank, what, cls)
+            k, d = GATH.index(what), dest(rank, what, cls)
             if late and b <= d < b + half:
                 g.wait_ge(T.sem.lg, 16)
                 late = False
@@ -135,15 +231,22 @@ def rank_program(g, core, T, topo):
             continue
         trs = []
         for blk in what:
-            k, d = BLOCKS.index(blk), dest(rank, blk, cls)
-            g.wait_ge(T.sem["g%d" % k], 16)
+            d = dest(rank, blk, cls)
+            if blk in COMP:
+                k = COMP.index(blk)
+                g.wait_ge(T.sem["cb%d" % k], 1)
+                src = T.cb[:, k * W:(k + 1) * W]
+            else:
+                k = GATH.index(blk)
+                g.wait_ge(T.sem["g%d" % k], 16)
+                src = T.gat[:, k * W:(k + 1) * W]
             to, m = hops[blk]
             rid, pid = topo.addr(to, core)
             if blk[0] == "x":
                 dst, sem = T.land[d], T.sem["hin%d" % (int(blk[1:]) // NHELP)]
             else:
                 dst, sem = T.land[rank], T.sem["arr%d" % rank]
-            trs.append((rid, pid, m, sem, T.gat[:, k * W:(k + 1) * W], dst))
+            trs.append((rid, pid, m, sem, src, dst))
             sent += len(bits(m))
         if len(trs) == 1:
             rid, pid, m, sem, src, dst = trs[0]
@@ -157,9 +260,9 @@ def rank_program(g, core, T, topo):
     for q, sem, order in ((g.sync, T.sem.sts, STORES["sync"]), (g.scalar, T.sem.sta, STORES["scalar"])):
         for blk in order:
             if blk == "own":
-                k = BLOCKS.index(blk)
-                q.wait_ge(T.sem["g%d" % k], 16)
-                q.dma_start(T.y[rank * CAP:(rank + 1) * CAP, :], T.gat[:, k * W:(k + 1) * W]).then_inc(sem, 16)
+                k = COMP.index(blk)
+                q.wait_ge(T.sem["cb%d" % k], 1)
+                q.dma_start(T.y[rank * CAP:(rank + 1) * CAP, :], T.cb[:, k * W:(k + 1) * W]).then_inc(sem, 16)
                 continue
             r = [s for s in range(N) if s != rank and dest(s, blk, cls) == rank][0]
             to, m = first_hops(r, cores, cls, topo)[blk]

@@ -6,12 +6,12 @@ WORLD = 256
 
 PLAN = [("g", "x0"), ("g", "x1"), ("g", "x2"), ("s", ["x0", "x1"]),
         ("g", "x3"), ("g", "s1"), ("s", ["x2", "x3"]),
-        ("g", "s2"), ("s", ["s1"]), ("s", ["s2"]), ("s", ["s3"])]
+        ("g", "own"), ("s", ["s1"]), ("s", ["s2"]), ("s", ["s3"])]
 GATH = [b for op, b in PLAN if op == "g"]
-COMP = ["s3", "own"]
+COMP = ["s2", "s3"]
 BLOCKS = GATH + COMP
 NHELP = 2
-STORES = {"sync": ["x0", "s1", "x2", "s3"], "scalar": ["x1", "x3", "s2", "own"]}
+STORES = {"sync": ["x0", "s1", "x2", "s3"], "scalar": ["x1", "own", "x3", "s2"]}
 
 NCH = 8
 CR = ROWS // NCH
@@ -19,6 +19,7 @@ SL = CR // 128
 CW = SL * W
 NB = 4
 H = W // 128
+NU = NCH * H
 OC = CAP // 16
 
 SCRATCH = {
@@ -28,6 +29,8 @@ SCRATCH = {
     "xt": ("sbuf", [128, H * ROWS], "bfloat16"),
     "gt": ("sbuf", [128, len(COMP) * W], "bfloat16"),
     "cb": ("sbuf", [128, len(COMP) * W], "bfloat16"),
+    "ones": ("sbuf", [128, 128], "float32"), "ramp": ("sbuf", [128, 128], "float32"), "trp": ("sbuf", [128, 128], "float32"),
+    "pcol": ("sbuf", [128, 1], "float32"),
     "iot": ("sbuf", [128, 128], "int32"), "iob": ("sbuf", [128, OC], "int32"),
     "t15": ("sbuf", [128, 128], "int32"), "m4": ("sbuf", [128, OC], "int32"),
     "ident": ("sbuf", [128, 128], "bfloat16"), "sel": ("sbuf", [128, 128], "float32"), "mhi": ("sbuf", [128, OC], "float32"),
@@ -39,11 +42,12 @@ SCRATCH = {
     "pb": ("psum", [128, len(COMP) * CW], "bfloat16"),
     "land": ("dram", [N, 128, W], "bfloat16"),
 }
-SEMAPHORES = (["lld", "lg", "sent", "sts", "sta", "cio", "cid", "va", "lm", "mo", "of"]
+SEMAPHORES = (["lld", "lg", "sent", "sts", "sta", "cid", "va", "lm", "mo", "of"]
               + ["g%d" % k for k in range(len(GATH))] + ["arr%d" % k for k in range(N)]
               + ["hin%d" % k for k in range(4 // NHELP)]
-              + ["%s%d" % (n, k) for n in ("xl", "tp", "ev") for k in range(NCH)]
-              + ["%s%d" % (n, k) for n in ("gq", "bt", "cb") for k in range(len(COMP))])
+              + ["xl%d" % k for k in range(NCH)] + ["%s%d" % (n, u) for n in ("tp", "ev") for u in range(NU)]
+              + ["gq%d" % k for k in range(len(COMP) * H)]
+              + ["%s%d" % (n, k) for n in ("bt", "cb") for k in range(len(COMP))])
 
 
 def bits(mask):
@@ -116,62 +120,88 @@ def first_hops(r, cores, cls, topo):
 def compute_way(g, T, lists):
     V, P, A, S = g.vector, g.tensor, AluOpType, T.sem
     nq = len(lists)
-    V.wait_ge(S["cio"], 2)
-    V.tensor_scalar(T.ident[:], T.iot[:], 128, None, A.is_equal).then_inc(S["cid"], 1)
-    V.tensor_scalar(T.t15[:], T.iot[:], 15, None, A.bitwise_and).then_inc(S["va"], 1)
-    V.tensor_scalar(T.m4[:], T.iob[:], 4, None, A.logical_shift_right).then_inc(S["va"], 1)
-    V.wait_ge(S["va"], 2)
-    V.tensor_scalar(T.sel[:], T.t15[:], 0, None, A.is_equal).then_inc(S["lm"], 1)
-    V.tensor_scalar(T.mhi[:], T.m4[:], 8, None, A.is_equal).then_inc(S["va"], 1)
-    V.wait_ge(S["lld"], 16)
-    V.wait_ge(S["lg"], 16)
-    V.tensor_scalar(T.t1[:], T.lsb[:], ROWS - CR, None, A.bitwise_and).then_inc(S["va"], 1)
-    V.tensor_scalar(T.t2[:], T.lsb[:], SL - 1, None, A.bitwise_and).then_inc(S["va"], 1)
-    V.tensor_scalar(T.t3[:], T.lsb[:], SL.bit_length() - 1, 127, A.logical_shift_right, A.bitwise_and).then_inc(S["va"], 1)
-    V.wait_ge(S["va"], 6)
-    V.tensor_scalar(T.f2[:], T.t2[:], 128, None, A.mult).then_inc(S["va"], 1)
-    V.tensor_tensor(T.f13[:], T.t1[:], T.t3[:], A.add).then_inc(S["va"], 1)
-    V.wait_ge(S["va"], 8)
-    V.tensor_tensor(T.off[:], T.f13[:], T.f2[:], A.add).then_inc(S["va"], 1)
-    V.wait_ge(S["va"], 9)
-    for q, d in enumerate(lists):
-        V.tensor_scalar(T.lmat[:, q * OC:(q + 1) * OC], T.mhi[:], T.off[:, d:d + 1], None, A.mult).then_inc(S["lm"], 1)
+    n = [0]
+
+    def v(ins):
+        ins.then_inc(S["va"], 1)
+        n[0] += 1
+
+    def vs():
+        V.wait_ge(S["va"], n[0])
+
+    v(V.memset(T.ones[:], 1.0))
+    vs()
+    v(V.tensor_tensor_scan(T.ramp[:], T.ones[:], T.ones[:], -1.0, A.mult, A.add))
+    vs()
+    v(V.transpose(T.trp[:], T.ramp[:]))
+    vs()
+    for a in range(4):
+        v(V.tensor_copy(T.pcol[32 * a:32 * a + 32, 0:1], T.trp[32 * a:32 * a + 32, 32 * a:32 * a + 1]))
+    vs()
+    V.tensor_scalar(T.ident[:], T.ramp[:], T.pcol[:, 0:1], None, A.is_equal).then_inc(S["cid"], 1)
+
+    def offsets():
+        v(V.tensor_scalar(T.iot[:], T.ramp[:], T.pcol[:, 0:1], 128, A.subtract, A.add))
+        v(V.tensor_scalar(T.iob[:], T.ramp[:, 0:OC], -16, T.pcol[:, 0:1], A.mult, A.add))
+        V.wait_ge(S["lld"], 16)
+        V.wait_ge(S["lg"], 16)
+        v(V.tensor_scalar(T.t1[:], T.lsb[:], ROWS - CR, None, A.bitwise_and))
+        v(V.tensor_scalar(T.t2[:], T.lsb[:], SL - 1, None, A.bitwise_and))
+        v(V.tensor_scalar(T.t3[:], T.lsb[:], SL.bit_length() - 1, 127, A.logical_shift_right, A.bitwise_and))
+        vs()
+        v(V.tensor_scalar(T.t15[:], T.iot[:], 15, None, A.bitwise_and))
+        v(V.tensor_scalar(T.m4[:], T.iob[:], 4, None, A.arith_shift_right))
+        v(V.tensor_scalar(T.f2[:], T.t2[:], 128, None, A.mult))
+        v(V.tensor_tensor(T.f13[:], T.t1[:], T.t3[:], A.add))
+        vs()
+        V.tensor_scalar(T.sel[:], T.t15[:], 0, None, A.is_equal).then_inc(S["lm"], 1)
+        v(V.tensor_scalar(T.mhi[:], T.m4[:], 0, None, A.is_equal))
+        v(V.tensor_tensor(T.off[:], T.f13[:], T.f2[:], A.add))
+        vs()
+        for q, d in enumerate(lists):
+            V.tensor_scalar(T.lmat[:, q * OC:(q + 1) * OC], T.mhi[:], T.off[:, d:d + 1], None, A.mult).then_inc(S["lm"], 1)
 
     P.wait_ge(S["cid"], 1)
     for k in range(NCH):
         P.wait_ge(S["xl%d" % k], 16)
-        if k >= NB:
-            P.wait_ge(S["ev%d" % (k - NB)], H)
         for h in range(H):
+            u = k * H + h
+            if u >= NB:
+                P.wait_ge(S["ev%d" % (u - NB)], 1)
             for s in range(SL):
-                o = (k % NB) * CW + (h * SL + s) * 128
+                o = (u % NB) * CW + s * 128
                 i = k * CW + s * W + h * 128
-                P.transpose(T.pt[:, o:o + 128], T.xs[:, i:i + 128], T.ident[:]).then_inc(S["tp%d" % k], 1)
-        if k == 1:
+                P.transpose(T.pt[:, o:o + 128], T.xs[:, i:i + 128], T.ident[:]).then_inc(S["tp%d" % u], 1)
+        if k == 3:
             P.wait_ge(S["lm"], 1 + nq)
             P.matmul(T.po[:, 0:nq * OC], T.sel[:], T.lmat[:], True, True).then_inc(S["mo"], 1)
-    for q in range(nq):
-        P.wait_ge(S["gq%d" % q], H)
-        for h in range(H):
+    for h in range(H):
+        for q in range(nq):
+            P.wait_ge(S["gq%d" % (q * H + h)], 1)
             P.transpose(T.pb[:, q * CW + h * 128:q * CW + (h + 1) * 128], T.gt[:, (q * H + h) * 128:(q * H + h + 1) * 128],
                         T.ident[:]).then_inc(S["bt%d" % q], 1)
 
-    for k in range(NCH):
-        V.wait_ge(S["tp%d" % k], H * SL)
-        for h in range(H):
-            V.tensor_copy(T.xt[:, h * ROWS + k * CR:h * ROWS + (k + 1) * CR],
-                          T.pt[:, (k % NB) * CW + h * CR:(k % NB) * CW + (h + 1) * CR]).then_inc(S["ev%d" % k], 1)
-        if k == 1:
-            V.wait_ge(S["mo"], 1)
-            V.tensor_copy(T.offs[:], T.po[:, 0:nq * OC]).then_inc(S["of"], 1)
-    for k in range(NCH):
-        V.wait_ge(S["ev%d" % k], H)
-    V.wait_ge(S["of"], 1)
-    for q in range(nq):
-        for h in range(H):
+    def picks(h):
+        for k in range(NCH):
+            V.wait_ge(S["ev%d" % (k * H + h)], 1)
+        for q in range(nq):
             V.tensor_copy(T.gt[:, (q * H + h) * 128:(q * H + h + 1) * 128],
                           T.xt[:, h * ROWS:(h + 1) * ROWS].indirect(T.offs[:, q * OC:(q + 1) * OC])
-                          ).then_inc(S["gq%d" % q], 1)
+                          ).then_inc(S["gq%d" % (q * H + h)], 1)
+
+    for u in range(NU):
+        k, h = u // H, u % H
+        V.wait_ge(S["tp%d" % u], SL)
+        V.tensor_copy(T.xt[:, h * ROWS + k * CR:h * ROWS + (k + 1) * CR],
+                      T.pt[:, (u % NB) * CW:(u % NB) * CW + CR]).then_inc(S["ev%d" % u], 1)
+        if u == 3:
+            offsets()
+        if u == 9:
+            V.wait_ge(S["mo"], 1)
+            V.tensor_copy(T.offs[:], T.po[:, 0:nq * OC]).then_inc(S["of"], 1)
+            V.wait_ge(S["of"], 1)
+        if k == NCH - 1:
+            picks(h)
     for q in range(nq):
         V.wait_ge(S["bt%d" % q], H)
         V.tensor_copy(T.cb[:, q * W:(q + 1) * W], T.pb[:, q * CW:q * CW + W]).then_inc(S["cb%d" % q], 1)
@@ -211,8 +241,6 @@ def rank_program(g, core, T, topo):
     for k in range(NCH):
         q = g.scalar if k % 2 == 0 else g.sync
         q.dma_start(T.xs[:, k * CW:(k + 1) * CW], T.x[CR * k:CR * (k + 1), :]).then_inc(T.sem["xl%d" % k], 16)
-    g.iota(T.iot[:], [[-1, 128]], 128, 1).then_inc(T.sem["cio"], 1)
-    g.iota(T.iob[:], [[-16, OC]], 128, 1).then_inc(T.sem["cio"], 1)
     compute_way(g, T, [dest(rank, blk, cls) for blk in COMP])
 
     g.wait_ge(T.sem.lld, 16)
@@ -260,9 +288,9 @@ def rank_program(g, core, T, topo):
     for q, sem, order in ((g.sync, T.sem.sts, STORES["sync"]), (g.scalar, T.sem.sta, STORES["scalar"])):
         for blk in order:
             if blk == "own":
-                k = COMP.index(blk)
-                q.wait_ge(T.sem["cb%d" % k], 1)
-                q.dma_start(T.y[rank * CAP:(rank + 1) * CAP, :], T.cb[:, k * W:(k + 1) * W]).then_inc(sem, 16)
+                k = GATH.index(blk)
+                q.wait_ge(T.sem["g%d" % k], 16)
+                q.dma_start(T.y[rank * CAP:(rank + 1) * CAP, :], T.gat[:, k * W:(k + 1) * W]).then_inc(sem, 16)
                 continue
             r = [s for s in range(N) if s != rank and dest(s, blk, cls) == rank][0]
             to, m = first_hops(r, cores, cls, topo)[blk]

from concourse.bass import DstId, RemoteDMATransfer, IndirectOffsetOnAxis
from concourse.mybir import AluOpType

N, ROWS, W, CAP = 8, 4096, 256, 128
WORLD = 256

PLAN = [("g", "x0"), ("g", "x1"), ("g", "x2"), ("s", ["x0", "x1"]),
        ("g", "x3"), ("g", "s1"), ("s", ["x2", "x3"]),
        ("g", "own"), ("s", ["s1"]), ("s", ["s2"]), ("s", ["s3"])]
GATH = [b for op, b in PLAN if op == "g"]
COMP = ["s2", "s3"]
BLOCKS = GATH + COMP
NHELP = 2
STORES = {"sync": ["x0", "s1", "x2", "s3"], "scalar": ["x1", "own", "x3", "s2"]}

NCH = 8
CR = ROWS // NCH
SL = CR // 128
CW = SL * W
NB = 4
H = W // 128
NU = NCH * H
OC = CAP // 16

SCRATCH = {
    "lsb": ("sbuf", [128, N], "int32"),
    "gat": ("sbuf", [128, len(GATH) * W], "bfloat16"),
    "xs": ("sbuf", [128, NCH * CW], "bfloat16"),
    "xt": ("sbuf", [128, H * ROWS], "bfloat16"),
    "gt": ("sbuf", [128, len(COMP) * W], "bfloat16"),
    "cb": ("sbuf", [128, len(COMP) * W], "bfloat16"),
    "ones": ("sbuf", [128, 128], "float32"), "ramp": ("sbuf", [128, 128], "float32"), "trp": ("sbuf", [128, 128], "float32"),
    "pcol": ("sbuf", [128, 1], "float32"),
    "iot": ("sbuf", [128, 128], "int32"), "iob": ("sbuf", [128, OC], "int32"),
    "t15": ("sbuf", [128, 128], "int32"), "m4": ("sbuf", [128, OC], "int32"),
    "ident": ("sbuf", [128, 128], "bfloat16"), "sel": ("sbuf", [128, 128], "float32"), "mhi": ("sbuf", [128, OC], "float32"),
    "t1": ("sbuf", [128, N], "int32"), "t2": ("sbuf", [128, N], "int32"), "t3": ("sbuf", [128, N], "int32"),
    "f2": ("sbuf", [128, N], "float32"), "f13": ("sbuf", [128, N], "float32"), "off": ("sbuf", [128, N], "float32"),
    "lmat": ("sbuf", [128, len(COMP) * OC], "float32"), "offs": ("sbuf", [128, len(COMP) * OC], "uint16"),
    "pt": ("psum", [128, NB * CW], "bfloat16"),
    "po": ("psum", [128, 512], "float32"),
    "pb": ("psum", [128, len(COMP) * CW], "bfloat16"),
    "land": ("dram", [N, 128, W], "bfloat16"),
}
SEMAPHORES = (["lld", "lg", "sent", "sts", "sta", "cid", "va", "lm", "mo", "of"]
              + ["g%d" % k for k in range(len(GATH))] + ["arr%d" % k for k in range(N)]
              + ["hin%d" % k for k in range(4 // NHELP)]
              + ["xl%d" % k for k in range(NCH)] + ["%s%d" % (n, u) for n in ("tp", "ev") for u in range(NU)]
              + ["gq%d" % k for k in range(len(COMP) * H)]
              + ["%s%d" % (n, k) for n in ("bt", "cb") for k in range(len(COMP))])


def bits(mask):
    return [1 << b for b in range(16) if (mask >> b) & 1]


def join(bs):
    m = 0
    for b in bs:
        m |= b
    return m


def classes(cores, topo):
    cls = []
    for r, c in enumerate(cores):
        for k in cls:
            if topo.may_write(cores[k[0]], c) and topo.may_write(c, cores[k[0]]):
                k.append(r)
                break
        else:
            cls.append([r])
    return cls


def dest(r, block, cls):
    mine = [k for k in cls if r in k][0]
    other = [k for k in cls if r not in k][0]
    if block == "own":
        return r
    k = int(block[1:])
    to = mine if block[0] == "s" else other
    return to[mine.index(r) ^ k]


def helpers(r, cores, cls, topo):
    c = cores[r]
    far = [cores[dest(r, b, cls)] for b in BLOCKS if b[0] == "x"]
    hs = [h for h in range(WORLD) if h != c and topo.host(h) == topo.host(c) and topo.chip(h) == topo.chip(c)
          and all(topo.may_write(h, f) for f in far)]
    hs = [h for h in hs if topo.die(h) != topo.die(c)] + [h for h in hs if topo.die(h) == topo.die(c)]
    return hs[:NHELP]


def first_hops(r, cores, cls, topo):
    c = cores[r]
    hs = helpers(r, cores, cls, topo)
    tgt = {}
    for b in BLOCKS:
        if b[0] == "x":
            tgt[b] = hs[int(b[1:]) % NHELP]
        elif b[0] == "s":
            tgt[b] = cores[dest(r, b, cls)]
    pool = None
    for t in tgt.values():
        pool = topo.mask(c, t) if pool is None else pool & topo.mask(c, t)
    pool = bits(pool)
    out = {}
    for op, bs in PLAN:
        if op != "s":
            continue
        per = 1
        while per * 2 * len(bs) <= len(pool):
            per *= 2
        for j, b in enumerate(bs):
            out[b] = (tgt[b], join(pool[j * per:(j + 1) * per]))
    return out


def compute_way(g, T, lists):
    V, P, A, S = g.vector, g.tensor, AluOpType, T.sem
    nq = len(lists)
    n = [0]

    def v(ins):
        ins.then_inc(S["va"], 1)
        n[0] += 1

    def vs():
        V.wait_ge(S["va"], n[0])

    v(V.memset(T.ones[:], 1.0))
    vs()
    v(V.tensor_tensor_scan(T.ramp[:], T.ones[:], T.ones[:], -1.0, A.mult, A.add))
    vs()
    v(V.transpose(T.trp[:], T.ramp[:]))
    vs()
    for a in range(4):
        v(V.tensor_copy(T.pcol[32 * a:32 * a + 32, 0:1], T.trp[32 * a:32 * a + 32, 32 * a:32 * a + 1]))
    vs()
    V.tensor_scalar(T.ident[:], T.ramp[:], T.pcol[:, 0:1], None, A.is_equal).then_inc(S["cid"], 1)

    def offsets():
        v(V.tensor_scalar(T.iot[:], T.ramp[:], T.pcol[:, 0:1], 128, A.subtract, A.add))
        v(V.tensor_scalar(T.iob[:], T.ramp[:, 0:OC], -16, T.pcol[:, 0:1], A.mult, A.add))
        V.wait_ge(S["lld"], 16)
        V.wait_ge(S["lg"], 16)
        v(V.tensor_scalar(T.t1[:], T.lsb[:], ROWS - CR, None, A.bitwise_and))
        v(V.tensor_scalar(T.t2[:], T.lsb[:], SL - 1, None, A.bitwise_and))
        v(V.tensor_scalar(T.t3[:], T.lsb[:], SL.bit_length() - 1, 127, A.logical_shift_right, A.bitwise_and))
        vs()
        v(V.tensor_scalar(T.t15[:], T.iot[:], 15, None, A.bitwise_and))
        v(V.tensor_scalar(T.m4[:], T.iob[:], 4, None, A.arith_shift_right))
        v(V.tensor_scalar(T.f2[:], T.t2[:], 128, None, A.mult))
        v(V.tensor_tensor(T.f13[:], T.t1[:], T.t3[:], A.add))
        vs()
        V.tensor_scalar(T.sel[:], T.t15[:], 0, None, A.is_equal).then_inc(S["lm"], 1)
        v(V.tensor_scalar(T.mhi[:], T.m4[:], 0, None, A.is_equal))
        v(V.tensor_tensor(T.off[:], T.f13[:], T.f2[:], A.add))
        vs()
        for q, d in enumerate(lists):
            V.tensor_scalar(T.lmat[:, q * OC:(q + 1) * OC], T.mhi[:], T.off[:, d:d + 1], None, A.mult).then_inc(S["lm"], 1)

    P.wait_ge(S["cid"], 1)
    for k in range(NCH):
        P.wait_ge(S["xl%d" % k], 16)
        for h in range(H):
            u = k * H + h
            if u >= NB:
                P.wait_ge(S["ev%d" % (u - NB)], 1)
            for s in range(SL):
                o = (u % NB) * CW + s * 128
                i = k * CW + s * W + h * 128
                P.transpose(T.pt[:, o:o + 128], T.xs[:, i:i + 128], T.ident[:]).then_inc(S["tp%d" % u], 1)
        if k == 3:
            P.wait_ge(S["lm"], 1 + nq)
            P.matmul(T.po[:, 0:nq * OC], T.sel[:], T.lmat[:], True, True).then_inc(S["mo"], 1)
    for h in range(H):
        for q in range(nq):
            P.wait_ge(S["gq%d" % (q * H + h)], 1)
            P.transpose(T.pb[:, q * CW + h * 128:q * CW + (h + 1) * 128], T.gt[:, (q * H + h) * 128:(q * H + h + 1) * 128],
                        T.ident[:]).then_inc(S["bt%d" % q], 1)

    def picks(h):
        for k in range(NCH):
            V.wait_ge(S["ev%d" % (k * H + h)], 1)
        for q in range(nq):
            V.tensor_copy(T.gt[:, (q * H + h) * 128:(q * H + h + 1) * 128],
                          T.xt[:, h * ROWS:(h + 1) * ROWS].indirect(T.offs[:, q * OC:(q + 1) * OC])
                          ).then_inc(S["gq%d" % (q * H + h)], 1)

    for u in range(NU):
        k, h = u // H, u % H
        V.wait_ge(S["tp%d" % u], SL)
        V.tensor_copy(T.xt[:, h * ROWS + k * CR:h * ROWS + (k + 1) * CR],
                      T.pt[:, (u % NB) * CW:(u % NB) * CW + CR]).then_inc(S["ev%d" % u], 1)
        if u == 3:
            offsets()
        if u == 9:
            V.wait_ge(S["mo"], 1)
            V.tensor_copy(T.offs[:], T.po[:, 0:nq * OC]).then_inc(S["of"], 1)
            V.wait_ge(S["of"], 1)
        if k == NCH - 1:
            picks(h)
    for q in range(nq):
        V.wait_ge(S["bt%d" % q], H)
        V.tensor_copy(T.cb[:, q * W:(q + 1) * W], T.pb[:, q * CW:q * CW + W]).then_inc(S["cb%d" % q], 1)


def rank_program(g, core, T, topo):
    cores = list(T.cores)
    cls = classes(cores, topo)
    rank = T.rank_of(core)

    if rank is None:
        own = [r for r in range(N) if topo.host(cores[r]) == topo.host(core) and topo.chip(cores[r]) == topo.chip(core)]
        if not own or core not in helpers(own[0], cores, cls, topo):
            return
        r = own[0]
        hops = first_hops(r, cores, cls, topo)
        sent = 0
        for b in BLOCKS:
            if b[0] != "x" or hops[b][0] != core:
                continue
            d = dest(r, b, cls)
            rid, pid = topo.addr(cores[d], core)
            m = topo.mask(core, cores[d])
            g.wait_ge(T.sem["hin%d" % (int(b[1:]) // NHELP)], len(bits(hops[b][1])))
            g.remote_dma(out_ap=T.land[r], in_ap=T.land[d], remote_sem=T.sem["arr%d" % r], local_sem=T.sem.sent,
                         pid=pid, routing_id=rid, dma_engine_mask=m)
            sent += len(bits(m))
        g.wait_ge(T.sem.sent, sent)
        return

    half = N // 2
    a = dest(rank, GATH[0], cls) // half * half
    assert dest(rank, GATH[1], cls) // half * half == a
    b = half - a
    g.sync.dma_start(T.lsb[:, a:a + half], T.l[:, a:a + half]).then_inc(T.sem.lld, 16)
    g.dma_start(T.lsb[:, b:b + half], T.l[:, b:b + half]).then_inc(T.sem.lg, 16)
    for k in range(NCH):
        q = g.scalar if k % 2 == 0 else g.sync
        q.dma_start(T.xs[:, k * CW:(k + 1) * CW], T.x[CR * k:CR * (k + 1), :]).then_inc(T.sem["xl%d" % k], 16)
    compute_way(g, T, [dest(rank, blk, cls) for blk in COMP])

    g.wait_ge(T.sem.lld, 16)
    late = True
    hops = first_hops(rank, cores, cls, topo)
    sent = 0
    for op, what in PLAN:
        if op == "g":
            k, d = GATH.index(what), dest(rank, what, cls)
            if late and b <= d < b + half:
                g.wait_ge(T.sem.lg, 16)
                late = False
            g.indirect_dma_start(T.gat[:, k * W:(k + 1) * W], None, T.x[:],
                                 IndirectOffsetOnAxis(ap=T.lsb[:, d:d + 1], axis=0),
                                 bounds_check=ROWS - 1).then_inc(T.sem["g%d" % k], 16)
            continue
        trs = []
        for blk in what:
            d = dest(rank, blk, cls)
            if blk in COMP:
                k = COMP.index(blk)
                g.wait_ge(T.sem["cb%d" % k], 1)
                src = T.cb[:, k * W:(k + 1) * W]
            else:
                k = GATH.index(blk)
                g.wait_ge(T.sem["g%d" % k], 16)
                src = T.gat[:, k * W:(k + 1) * W]
            to, m = hops[blk]
            rid, pid = topo.addr(to, core)
            if blk[0] == "x":
                dst, sem = T.land[d], T.sem["hin%d" % (int(blk[1:]) // NHELP)]
            else:
                dst, sem = T.land[rank], T.sem["arr%d" % rank]
            trs.append((rid, pid, m, sem, src, dst))
            sent += len(bits(m))
        if len(trs) == 1:
            rid, pid, m, sem, src, dst = trs[0]
            g.remote_dma(out_ap=dst, in_ap=src, remote_sem=sem, local_sem=T.sem.sent, pid=pid, routing_id=rid,
                         dma_engine_mask=m)
        else:
            g.remote_dma_fused([RemoteDMATransfer(dst_ids=[DstId(rid=rid, pnc=pid)], dma_engine_mask=m, remote_sem=sem,
                                                  src=src, dst=dst) for rid, pid, m, sem, src, dst in trs],
                               local_sem=T.sem.sent)

    for q, sem, order in ((g.sync, T.sem.sts, STORES["sync"]), (g.scalar, T.sem.sta, STORES["scalar"])):
        for blk in order:
            if blk == "own":
                k = GATH.index(blk)
                q.wait_ge(T.sem["g%d" % k], 16)
                q.dma_start(T.y[rank * CAP:(rank + 1) * CAP, :], T.gat[:, k * W:(k + 1) * W]).then_inc(sem, 16)
                continue
            r = [s for s in range(N) if s != rank and dest(s, blk, cls) == rank][0]
            to, m = first_hops(r, cores, cls, topo)[blk]
            if blk[0] == "x":
                m = topo.mask(to, core)
            q.wait_ge(T.sem["arr%d" % r], len(bits(m)))
            q.dma_start(T.y[r * CAP:(r + 1) * CAP, :], T.land[r]).then_inc(sem, 16)
    g.wait_ge(T.sem.sent, sent)
    g.wait_ge(T.sem.sts, 16 * len(STORES["sync"]))
    g.wait_ge(T.sem.sta, 16 * len(STORES["scalar"]))
